import numpy as np, ml_dtypes
CORES = [7,39,87,119,135,167,215,247,263,295,343,375,391,423,471,503]
N = 16
import mx_ref
NC, ROOT = 128, 11
A = np.float32(0.0125)
BF = ml_dtypes.bfloat16
def cut(t, i, w=512):
    return t[:, w * i:w * i + w]
def tile(rs):
    return np.stack(rs, axis=2).reshape(128, -1).astype(BF)
def pk(c, s, i=0):
    return (np.ascontiguousarray(c[:, 512 * i:512 * i + 512]), mx_ref.live(s[:, 128 * i:128 * i + 128]))
def raw(rng):
    def f(*shape):
        return mx_ref.flush((rng.standard_normal(shape, dtype=np.float32) * np.exp2(rng.integers(-2, 3, shape[:-1] + (1,)))).astype(BF))
    return {"q": f(N, 128, 4 * NC), "k": f(N, 128, 4 * 512), "v": f(N, 128, 512)}
def raw_blocks(rng):
    d = raw(rng)
    for k in ("v",): d[k] = mx_ref.spread(d[k], rng, 4)
    for k in ("q", "k"): d[k] = mx_ref.spread(d[k], rng, 1)
    return d
def raw_wide(rng):
    d = raw(rng)
    for k in ("v",): d[k] = mx_ref.flush((d[k].astype(np.float32) * np.exp2(rng.integers(-8, 9, (N, 1, 1))).astype(np.float32)).astype(BF))
    return d
def raw_sharp(rng):
    d = raw(rng); v = d["q"].astype(np.float32).reshape(N, 128, -1, 4)
    d["q"] = mx_ref.flush((v * np.exp2(rng.integers(-2, 4, (N, 1, v.shape[2], 1))).astype(np.float32)).reshape(d["q"].shape).astype(BF))
    return d
def raw_offset(rng):
    d = raw(rng); v = d["k"].astype(np.float32).reshape(N, 128, -1, 4)
    d["k"] = mx_ref.flush((v + 12 * rng.standard_normal((1, 128, 1, 4), dtype=np.float32)).reshape(d["k"].shape).astype(BF))
    return d
def pack(d, rng):
    o = {"q": d["q"]}
    for m in ("k", "v"):
        t = d[m]; c = np.zeros(t.shape, np.uint8); s = np.zeros((N, 128, t.shape[2] // 4), np.uint8)
        for r in range(N):
            for i in range(t.shape[2] // 512):
                a, b = mx_ref.quantize(cut(t[r], i)); c[r][:, 512 * i:512 * i + 512] = a; s[r][:, 128 * i:128 * i + 128] = mx_ref.plane(b, rng)
        o[m + "c"], o[m + "s"] = c, s
    return o
def setup_inputs(rng):
    return pack(raw(rng), rng)
def setup_inputs_blocks(rng):
    return pack(raw_blocks(rng), rng)
def setup_inputs_offset(rng):
    return pack(raw_offset(rng), rng)
def setup_inputs_sharp(rng):
    return pack(raw_sharp(rng), rng)
def setup_inputs_wide(rng):
    return pack(raw_wide(rng), rng)
def reference(q, kc, ks, vc, vs, own=None):
    ONE = mx_ref.quantize(np.ones((128, 512), BF)); Q = mx_ref.quantize(q[ROOT])
    S = [[mx_ref.matmul(pk(kc[j], ks[j], b), Q) * A for b in range(4)] for j in range(N)]
    lo = np.stack([np.max(s, axis=(0, 1))[None] for s in S]); hi = np.broadcast_to(lo.max(axis=0) + 8, lo.shape).copy()
    c = lo if own is None else own["c"]
    p = np.stack([tile([np.exp(np.maximum(s - c[j], -20).astype(np.float64)).astype(np.float32) for s in S[j]]) for j in range(N)])
    use = p if own is None else own["p"]
    e = np.exp((c - c.max(axis=0)).astype(np.float64))[:, 0]; wlo = np.zeros((N, N, NC), np.float32); whi = np.ones((N, N, NC), np.float32); wlo[ROOT] = e * (1 - 4e-5); whi[ROOT] = e * (1 + 4e-5)
    w = np.zeros((N, N, NC), np.float32); w[ROOT] = e
    if own is not None: w = own["w"]
    num = den = 0
    for j in range(N):
        P = mx_ref.quantize(use[j])
        num = num + w[ROOT][j].astype(np.float64) * mx_ref.matmul(pk(vc[j], vs[j]), P); den = den + w[ROOT][j].astype(np.float64) * mx_ref.matmul(ONE, P)
    o = np.full((N, 128, NC), np.nan, np.float32); o[ROOT] = (num / den).astype(np.float32)
    return {"c": c, "c__lo": lo, "c__hi": hi, "p": p, "w": w, "w__lo": wlo, "w__hi": whi, "o": o}

import numpy as np
import math
from concourse.bass import DstId, RemoteDMATransfer
from concourse.mybir import dt, AluOpType, AxisListType, ActivationFunctionType

NR = 16
NQ = 128
NA = NQ + 1
SL = 132
SCALE = 0.0125
FLOOR = -20.0
MARGIN = 0.5

SCRATCH = {
    "qb": ("sbuf", [128, 512], "bfloat16"),
    "qc": ("sbuf", [128, 128], "float8_e4m3fn_x4"),
    "qs": ("sbuf", [128, 128], "uint8"),
    "kcd": ("sbuf", [128, 512], "float8_e4m3fn_x4"),
    "ksc": ("sbuf", [128, 512], "uint8"),
    "voc": ("sbuf", [128, 256], "float8_e4m3fn_x4"),
    "vos": ("sbuf", [128, 256], "uint8"),
    "one": ("sbuf", [128, 512], "bfloat16"),
    "pst": ("psum", [128, 512], "float32"),
    "pss": ("psum", [128, 2048], "float32"),
    "psa": ("psum", [128, 512], "float32"),
    "red": ("sbuf", [128, 4], "float32"),
    "fac": ("sbuf", [128, 32], "float32"),
    "n20": ("sbuf", [128, 4], "float32"),
    "e20": ("sbuf", [128, 4], "float32"),
    "wc": ("sbuf", [128, 32], "float32"),
    "cb": ("sbuf", [128, 128], "float32"),
    "x": ("sbuf", [128, 512], "float32"),
    "y": ("sbuf", [128, 512], "float32"),
    "ex": ("sbuf", [128, 512], "float32"),
    "pt": ("sbuf", [128, 512], "bfloat16"),
    "pc": ("sbuf", [128, 128], "float8_e4m3fn_x4"),
    "psc": ("sbuf", [128, 128], "uint8"),
    "res": ("sbuf", [128, SL], "float32"),
    "fl": ("sbuf", [128, SL], "float32"),
    "fcl": ("sbuf", [128, 4], "float32"),
    "cl": ("sbuf", [128, 4 * NR], "float32"),
    "rl": ("sbuf", [128, SL * NR], "float32"),
    "tm": ("sbuf", [128, SL * NR], "float32"),
    "mx": ("sbuf", [128, 4], "float32"),
    "dl": ("sbuf", [128, NR], "float32"),
    "wt": ("sbuf", [128, 32], "float32"),
    "wtt": ("sbuf", [128, 128], "float32"),
    "acc": ("sbuf", [128, SL], "float32"),
    "rcp": ("sbuf", [128, 4], "float32"),
    "ot": ("sbuf", [128, 128], "float32"),
    "z": ("sbuf", [128, 128], "float32"),
}
SEMAPHORES = (["qld", "kld", "vld", "q", "ms", "one", "e20", "t", "red", "wc", "tr", "cp1", "cp2", "pm", "pq", "a", "r",
               "loc", "out", "cl", "fc", "fr", "oc", "mx", "dl", "wt", "wtr", "rcp", "ot"]
              + ["%s%d" % (s, b) for s in ("s", "x", "y", "e", "z") for b in range(4)]
              + ["%s%d" % (s, j) for s in ("ra", "tm", "ac") for j in range(NR)])


def _plan(cores, root, topo):
    n = len(cores)
    rc = cores[root]

    def rack(j):
        return topo.rack(topo.host(cores[j]))

    def cabled(i, j):
        return rack(i) != rack(j) and topo.may_write(cores[i], cores[j]) and topo.chip(cores[i]) == topo.chip(cores[j])

    others = [j for j in range(n) if j != root]
    far = [j for j in others if not topo.may_write(rc, cores[j])]
    near = [j for j in others if j not in far]
    home = [j for j in near if rack(j) == rack(root)]
    away = [j for j in near if j not in home]
    hub = [j for j in away if cabled(root, j)][0]
    back = {f: [x for x in home if cabled(f, x)][0] for f in far}
    rest = [j for j in away if j != hub]
    by_cable, by_hub = far[:len(far) // 2], far[len(far) // 2:][::-1]
    kids = {j: [] for j in range(n)}
    kids[hub] = by_hub + rest
    for f in by_cable:
        kids[back[f]] = [f]
    gates = [back[f] for f in far]
    kids[root] = [hub] + gates + [j for j in home if j not in gates]
    up = {j: (back[j] if j in far else root) for j in others}
    order = [root] + kids[root][1:] + [hub] + rest[:2] + by_hub[:1] + rest[2:] + by_hub[1:] + by_cable
    return kids, up, order


def rank_program(g, core, T, topo):
    rank = T.rank_of(core)
    if rank is None:
        return
    cores = [int(c) for c in T.cores]
    n = len(cores)
    root = int(T.root)
    kids, up, order = _plan(cores, root, topo)
    isroot = rank == root
    v, a, pe, sy = g.vector, g.scalar, g.tensor, g.sync
    Alu, Act, X = AluOpType, ActivationFunctionType, AxisListType.X
    tot = {}

    def S(name):
        return T.sem[name]

    def expect(name, k):
        tot[name] = tot.get(name, 0) + k

    def inc(ins, name, k=1):
        ins.then_inc(S(name), k)
        expect(name, k)

    def engines(i, j):
        return bin(topo.mask(cores[i], cores[j])).count("1")

    def send(out_ap, in_ap, j, sem):
        rid, pid = topo.addr(cores[j], core)
        g.remote_dma(out_ap=out_ap, in_ap=in_ap, remote_sem=S(sem), local_sem=S("loc"), pid=pid, routing_id=rid,
                     dma_engine_mask=topo.mask(core, cores[j]))
        expect("loc", engines(rank, j))

    def blk(b):
        return slice(NQ * b, NQ * b + NQ)

    def q32(k):
        return slice(32 * k, 32 * k + 32)

    guests = [f for f in up if up[f] == rank and not isroot]
    if not isroot:
        parent = [i for i in kids if rank in kids[i]][0]
        expect("q", 2 * engines(parent, rank))
    else:
        for j in up:
            last = j if up[j] == root else up[j]
            expect("cl", engines(last, root))
            expect("ra%d" % j, engines(last, root))
    for f in guests:
        expect("fc", engines(f, rank))
        expect("fr", engines(f, rank))

    if isroot:
        inc(sy.dma_start(T.qb[:], T.q[:, :]), "qld", 16)
    inc(sy.dma_start(T.kcd[:].bitcast(dt.uint8), T.kc[:, :]), "kld", 16)
    inc(a.dma_start(T.ksc[:], T.ks[:, :]), "kld", 16)
    inc(sy.dma_start(T.voc[:, 0:128].bitcast(dt.uint8), T.vc[:, :]), "vld", 16)
    inc(a.dma_start(T.vos[:, 0:128], T.vs[:, :]), "vld", 16)

    inc(v.memset(T.one[:], 1.0), "ms")
    inc(v.memset(T.fac[:], SCALE), "ms")
    inc(v.memset(T.n20[:], FLOOR), "ms")
    if isroot:
        inc(v.memset(T.wt[:], 0.0), "ms")
    else:
        inc(v.memset(T.wtt[0:n, :], 0.0), "ms")
    nms = tot["ms"]
    v.wait_ge(S("ms"), nms)
    inc(v.quantize_mx(T.voc[:, 128:256], T.vos[:, 128:256], T.one[:]), "one")
    a.wait_ge(S("ms"), nms)
    inc(a.activation(T.e20[:, 0:1], T.n20[:, 0:1], Act.Exp), "e20")
    if not isroot:
        sy.wait_ge(S("ms"), nms)
        inc(sy.dma_start(T.w[:, :], T.wtt[0:n, 0:NQ]), "out", 16)

    if isroot:
        v.wait_ge(S("qld"), 16)
        inc(v.quantize_mx(T.qc[:], T.qs[:], T.qb[:]), "q", 16)
    nq = tot["q"]
    if kids[rank]:
        g.wait_ge(S("q"), nq)
        for j in kids[rank]:
            send(T.qc[:].bitcast(dt.uint8), T.qc[:].bitcast(dt.uint8), j, "q")
            send(T.qs[:], T.qs[:], j, "q")

    pe.wait_ge(S("kld"), 32)
    pe.wait_ge(S("q"), nq)
    inc(pe.matmul_mx(T.pst[:, 0:512], T.qc[:], T.qs[:], T.kcd[:], T.ksc[:], True, True), "t")
    for b in range(4):
        inc(pe.matmul_mx(T.pss[:, 512 * b:512 * b + NQ], T.kcd[:, blk(b)], T.ksc[:, blk(b)], T.qc[:], T.qs[:], True, True),
            "s%d" % b)
    for b in range(4):
        a.wait_ge(S("s%d" % b), 1)
        inc(a.activation(T.x[:, blk(b)], T.pss[:, 512 * b:512 * b + NQ], Act.Copy, scale=SCALE), "x%d" % b)

    v.wait_ge(S("t"), 1)
    inc(v.tensor_reduce(T.red[:, 0:1], T.pst[:, 0:512], X, Alu.max), "red")
    v.wait_ge(S("red"), 1)
    inc(v.tensor_scalar(T.wc[:, 0:32], T.fac[:, 0:32], T.red[:, 0:1], MARGIN, Alu.mult, Alu.add), "wc")
    v.wait_ge(S("wc"), 1)
    for k in range(4):
        inc(v.transpose(T.cb[0:32, q32(k)], T.wc[q32(k), 0:32]), "tr")
    if isroot:
        inc(v.tensor_copy(T.cl[:, 4 * rank:4 * rank + 1], T.wc[:, 0:1]), "oc")
    v.wait_ge(S("tr"), 4)
    inc(v.tensor_copy(T.cb[32:64, :], T.cb[0:32, :]), "cp1")
    v.wait_ge(S("cp1"), 1)
    inc(v.tensor_copy(T.cb[64:128, :], T.cb[0:64, :]), "cp2")
    v.wait_ge(S("cp2"), 1)
    v.wait_ge(S("e20"), 1)
    sy.wait_ge(S("tr"), 4)
    inc(sy.dma_start(T.c[:, :], T.cb[0:1, 0:NQ]), "out", 16)

    def sub(b):
        v.wait_ge(S("x%d" % b), 1)
        inc(v.tensor_tensor(T.y[:, blk(b)], T.x[:, blk(b)], T.cb[:, :], Alu.subtract), "y%d" % b)

    def top(b):
        v.wait_ge(S("e%d" % b), 1)
        inc(v.tensor_scalar(T.pt[:, b:512:4], T.ex[:, blk(b)], T.e20[:, 0:1], None, Alu.max), "pm")

    for b in range(4):
        a.wait_ge(S("y%d" % b), 1)
        inc(a.activation(T.ex[:, blk(b)], T.y[:, blk(b)], Act.Exp), "e%d" % b)
    sub(0), sub(1), top(0), sub(2), top(1), sub(3), top(2), top(3)
    v.wait_ge(S("pm"), 4)
    inc(v.quantize_mx(T.pc[:], T.psc[:], T.pt[:]), "pq")
    sy.wait_ge(S("pm"), 4)
    inc(sy.dma_start(T.p[:, :], T.pt[:]), "out", 16)

    pe.wait_ge(S("vld"), 32)
    pe.wait_ge(S("one"), 1)
    pe.wait_ge(S("pq"), 1)
    inc(pe.matmul_mx(T.psa[:, 0:NQ + 2], T.pc[:], T.psc[:], T.voc[:, 0:NQ + 2], T.vos[:, 0:NQ + 2], True, True), "a")
    v.wait_ge(S("a"), 1)
    inc(v.tensor_copy(T.res[:, 0:NA], T.psa[:, 0:NA]), "r")

    if not isroot:
        direct = up[rank] == root
        g.wait_ge(S("wc"), 1)
        send(T.cl[:, 4 * rank:4 * rank + 1] if direct else T.fcl[:, 0:1], T.wc[:, 0:1], up[rank], "cl" if direct else "fc")
        g.wait_ge(S("r"), 1)
        send(T.rl[:, SL * rank:SL * rank + NA] if direct else T.fl[:, 0:NA], T.res[:, 0:NA], up[rank],
             ("ra%d" % rank) if direct else "fr")
        for f in guests:
            g.wait_ge(S("fc"), tot["fc"])
            send(T.cl[:, 4 * f:4 * f + 1], T.fcl[:, 0:1], root, "cl")
            g.wait_ge(S("fr"), tot["fr"])
            send(T.rl[:, SL * f:SL * f + NA], T.fl[:, 0:NA], root, "ra%d" % f)

    if isroot:
        v.wait_ge(S("oc"), 1)
        v.wait_ge(S("cl"), tot["cl"])
        inc(v.tensor_reduce(T.mx[:, 0:1], T.cl[:, 0:4 * n:4], X, Alu.max), "mx")
        v.wait_ge(S("mx"), 1)
        inc(v.tensor_scalar(T.dl[:, 0:n], T.cl[:, 0:4 * n:4], T.mx[:, 0:1], None, Alu.subtract), "dl")
        a.wait_ge(S("dl"), 1)
        inc(a.activation(T.wt[:, 0:n], T.dl[:, 0:n], Act.Exp), "wt")
        a.wait_ge(S("wt"), 1)
        v.wait_ge(S("wt"), 1)
        for k in range(4):
            inc(v.transpose(T.wtt[0:32, q32(k)], T.wt[q32(k), 0:32]), "wtr")
        sy.wait_ge(S("wtr"), 4)
        inc(sy.dma_start(T.w[:, :], T.wtt[0:n, 0:NQ]), "out", 16)

        def slot(j):
            return slice(SL * j, SL * j + NA)

        for j in order:
            if j == root:
                a.wait_ge(S("r"), 1)
                src = T.res[:, 0:NA]
            else:
                a.wait_ge(S("ra%d" % j), tot["ra%d" % j])
                src = T.rl[:, slot(j)]
            inc(a.activation(T.tm[:, slot(j)], src, Act.Copy, scale=T.wt[:, j:j + 1]), "tm%d" % j)
        for i in range(1, n):
            j = order[i]
            v.wait_ge(S("tm%d" % j), 1)
            if i == 1:
                v.wait_ge(S("tm%d" % order[0]), 1)
                first = T.tm[:, slot(order[0])]
            else:
                v.wait_ge(S("ac%d" % (i - 1)), 1)
                first = T.acc[:, 0:NA]
            inc(v.tensor_tensor(T.acc[:, 0:NA], first, T.tm[:, slot(j)], Alu.add), "ac%d" % i)
        v.wait_ge(S("ac%d" % (n - 1)), 1)
        inc(v.reciprocal(T.rcp[:, 0:1], T.acc[:, NQ:NA]), "rcp")
        v.wait_ge(S("rcp"), 1)
        inc(v.tensor_scalar(T.ot[:, 0:NQ], T.acc[:, 0:NQ], T.rcp[:, 0:1], None, Alu.mult), "ot")
        v.wait_ge(S("ot"), 1)
        for b in range(4):
            for k in range(4):
                inc(v.transpose(T.z[q32(b), q32(k)], T.ot[q32(k), q32(b)]), "z%d" % b)
            dq = sy if b % 2 == 0 else a
            dq.wait_ge(S("z%d" % b), 4)
            inc(dq.dma_start(T.o[q32(b), :], T.z[q32(b), :]), "out", 16)

    for name in sorted(tot):
        g.wait_ge(S(name), tot[name])
